import numpy as np
import ml_dtypes


def mxq(x, axis, fmt="e4m3"):
    dtype, down = {"e4m3": (ml_dtypes.float8_e4m3fn, 7), "e5m2": (ml_dtypes.float8_e5m2, 14)}[fmt]
    v = np.moveaxis(np.asarray(x, np.float32).astype(ml_dtypes.bfloat16).astype(np.float64), axis, -1)
    blocks = v.reshape(v.shape[:-1] + (-1, 32))
    amax = np.abs(blocks).max(-1, keepdims=True)
    byte = np.maximum(np.where(amax > 0, np.frexp(amax)[1] - 1 + 127, 0) - down, 1)
    scale = np.exp2(byte - 127.0)
    codes = (blocks / scale).astype(np.float32).astype(dtype).astype(np.float64)
    return np.moveaxis((codes * scale).reshape(v.shape), -1, axis)


WIDE = False


def mx_kscale(k):
    if not WIDE:
        return np.ones(k)
    levels = np.array([10, -10, 5, -5, 0])
    if k % 512:
        return np.exp2(np.random.permutation(np.resize(levels, k // 32))).repeat(32)
    a = np.empty((k // 512, 16))
    for p in range(k // 512):
        a[p, :8] = np.random.permutation(np.resize(levels, 8))
        for g in range(8):
            far = levels[np.abs(levels - a[p, g]) >= 10]
            a[p, g + 8] = far[np.random.randint(len(far))]
    return np.exp2(a.ravel()).repeat(32)


def f64(x):
    return np.asarray(x).astype(np.float64)


def striped8(idx):
    return np.asarray(idx).reshape(8, -1, 16).transpose(0, 2, 1).reshape(128, -1).astype(np.uint16)


def unstriped8(offs):
    return offs.reshape(8, 16, -1).transpose(0, 2, 1).reshape(8, -1).astype(np.int64)


def pick8(x, idx, run):
    r = np.arange(len(x))
    return x[r[:, None], idx[r % (8 * run) // run]]


E2M1 = np.array([0.0, 0.5, 1.0, 1.5, 2.0, 3.0, 4.0, 6.0, -0.0, -0.5, -1.0, -1.5, -2.0, -3.0, -4.0, -6.0])


def pack_weight(w, fmt):
    k, n = w.shape
    w = f64(np.asarray(w, np.float32).astype(ml_dtypes.bfloat16)).reshape(k // 32, 32, n)
    amax = np.abs(w).max(1)
    if fmt == "e4m3":
        byte = np.frexp(amax)[1] - 1 + 127 - 7
    else:
        mant, ex = np.frexp(amax / 6.0)
        byte = np.where(mant > 0.5, ex, ex - 1) + 127
    byte = np.clip(np.where(amax > 0, byte, 1), 1, 254)
    scaled = (w * np.exp2(127.0 - byte)[:, None, :]).reshape(k, n).astype(np.float32)
    by_word = np.ascontiguousarray(scaled.reshape(k // 512, 128, 4, n).transpose(0, 1, 3, 2))
    if fmt == "e4m3":
        words = by_word.astype(ml_dtypes.float8_e4m3fn).view(np.uint8)
    else:
        c = by_word.astype(ml_dtypes.float4_e2m1fn).view(np.uint8) & 0xF
        words = (c[..., 0::2] | (c[..., 1::2] << 4)).reshape(k // 512, 128, 2 * n)
    return np.ascontiguousarray(words), np.ascontiguousarray(byte.astype(np.uint8).reshape(k // 512, 16, n))


def unpack_weight(words, scales, fmt):
    g, _, n = scales.shape
    words = np.ascontiguousarray(words).reshape(g, 128, n, -1)
    if fmt == "e4m3":
        vals = words.view(ml_dtypes.float8_e4m3fn).astype(np.float64)
    else:
        nib = np.empty((g, 128, n, 4), np.uint8)
        nib[..., 0::2] = words & 0xF
        nib[..., 1::2] = words >> 4
        vals = E2M1[nib]
    vals = vals * np.repeat(np.exp2(scales.astype(np.float64) - 127.0), 8, axis=1)[..., None]
    return vals.transpose(0, 1, 3, 2).reshape(g * 512, n)


D, T, I, Q = 512, 1024, 512, 128


def setup_inputs():
    n = np.random.standard_normal
    idx = np.stack([np.random.permutation(T)[:I] for _ in range(8)])
    idx2 = np.stack([np.random.permutation(T)[:I] for _ in range(8)])
    idx4 = np.stack([np.random.permutation(T)[:I] for _ in range(8)])
    fd = mx_kscale(D)
    keysp = pack_weight(n((D, T)) / fd[:, None], "e4m3")
    return {
        "query": (n((D, Q)) * 1.0 / np.sqrt(D) * fd[:, None]).astype(np.float32),
        "query2": (n((D, Q)) * 1.0 / np.sqrt(D) * fd[:, None]).astype(np.float32),
        "keys_words": keysp[0],
        "keys_scales": keysp[1],
        "lam": (np.random.uniform(1.0, 3.0, (Q, 1))).astype(np.float32),
        "sharp": (np.random.uniform(1.5, 3.0, (Q, 1))).astype(np.float32),
        "share": (np.random.uniform(0.5, 0.9, (Q, 1))).astype(np.float32),
        "old": (np.random.uniform(0.0, 2.0, (Q, T))).astype(np.float32),
        "gainm": (np.random.uniform(0.5, 1.5, (Q, I))).astype(np.float32),
        "offs": striped8(idx),
        "offs2": striped8(idx2),
        "offs4": striped8(idx4),
    }


def reference(query, query2, keys_words, keys_scales, lam, sharp, share, old, gainm, offs, offs2, offs4):
    idx = unstriped8(offs)
    idx2 = unstriped8(offs2)
    idx4 = unstriped8(offs4)
    keysu = unpack_weight(keys_words, keys_scales, "e4m3")
    queryq = mxq(f64(query), 0, "e4m3")
    a = queryq.T @ keysu
    query2q = mxq(f64(query2), 0, "e4m3")
    b = query2q.T @ keysu
    la = np.square(pick8(a, idx, 16)) + np.square(pick8(b, idx, 16))
    lb = np.square(pick8(a, idx2, 16)) + np.square(pick8(b, idx2, 16))
    s = (pick8(a, idx, 16) * pick8(a, idx2, 16) + pick8(b, idx, 16) * pick8(b, idx2, 16)) / np.sqrt(la * lb + 0.5) * f64(lam)
    p = np.exp(s - np.max(s, axis=1, keepdims=True))
    r = p / np.sum(p, axis=1, keepdims=True)
    s2 = s * f64(sharp)
    p2 = np.exp(s2 - np.max(s2, axis=1, keepdims=True))
    r2 = p2 / np.sum(p2, axis=1, keepdims=True)
    w = r * f64(share) - r2 * (1.0 - f64(share))
    ws = w * f64(gainm) * 256.0
    wf = np.zeros((Q, T))
    wf[np.arange(Q)[:, None], idx4[np.arange(Q) % 128 // 16]] = ws
    y = f64(old) + wf
    return y

@@ -1,0 +1,165 @@
+from contextlib import ExitStack
+
+import concourse.mybir as mybir
+
+F32 = mybir.dt.float32
+BF16 = mybir.dt.bfloat16
+I32 = mybir.dt.int32
+U32 = mybir.dt.uint32
+U16 = mybir.dt.uint16
+U8 = mybir.dt.uint8
+FP8X4 = mybir.dt.float8_e4m3fn_x4
+ALU = mybir.AluOpType
+ACT = mybir.ActivationFunctionType
+AX = mybir.AxisListType
+
+P = 128
+PACK = 4
+D, T, I, Q = 512, 1024, 512, 128
+HALF = T // 2
+
+FLOPS = 2 * 2 * D * Q * T
+
+
+def tile_attend_planecos_twoheats_moved_heads_kernel(
+    tc, query, query2, keys_words, keys_scales, lam, sharp, share, old, gainm, offs, offs2, offs4, out
+):
+    nc = tc.nc
+    with ExitStack() as ctx:
+        pool = ctx.enter_context(tc.tile_pool(name="held", bufs=1))
+        psum = ctx.enter_context(tc.psum_pool(name="psum", bufs=1))
+
+        def sb(name, shape, dtype=F32):
+            return pool.tile(shape, dtype, name=name, align_bytes=64)
+
+        key_scales = sb("key_scales", [P, T], U8)
+        for quad in range(4):
+            nc.scalar.dma_start(
+                out=key_scales[32 * quad : 32 * quad + 4, :].bitcast(I32),
+                in_=keys_scales[0, 4 * quad : 4 * quad + 4, :].bitcast(I32),
+            )
+        key_bytes = keys_words[0].rearrange("p n t -> p (n t)")
+        raw = [sb("raw_a", [P, PACK, Q]), sb("raw_b", [P, PACK, Q])]
+        key_codes = [sb("key_codes_lo", [P, HALF], U32), sb("key_codes_hi", [P, HALF], U32)]
+        for h, src in enumerate((query, query2)):
+            nc.sync.dma_start(out=raw[h][:], in_=src.rearrange("(p j) q -> p j q", j=PACK))
+            nc.sync.dma_start(
+                out=key_codes[h][:].bitcast(I32),
+                in_=key_bytes[:, h * HALF * PACK : (h + 1) * HALF * PACK].bitcast(I32),
+            )
+        list1 = pool.tile([P, I // 16], U16, name="list1")
+        list2 = pool.tile([P, I // 16], U16, name="list2")
+        list4 = pool.tile([P, I // 16], U16, name="list4")
+        nc.sync.dma_start(list1[:], offs)
+        nc.sync.dma_start(list2[:], offs2)
+        gain = sb("gain", [P, I])
+        nc.sync.dma_start(out=gain[:], in_=gainm)
+        nc.sync.dma_start(list4[:], offs4)
+        old_sb = sb("old_sb", [P, T])
+        nc.sync.dma_start(out=old_sb[:], in_=old)
+        share_col = sb("share_col", [P, 1])
+        lam_col = sb("lam_col", [P, 1])
+        sharp_col = sb("sharp_col", [P, 1])
+        nc.gpsimd.dma_start(out=share_col[:], in_=share)
+        nc.gpsimd.dma_start(out=lam_col[:], in_=lam)
+        nc.gpsimd.dma_start(out=sharp_col[:], in_=sharp)
+
+        placed = sb("placed", [P, T])
+        nc.vector.memset(placed[:], 0.0)
+        half_col = sb("half_col", [P, 1])
+        nc.vector.memset(half_col[:], 0.5)
+
+        q_codes, q_scales = [], []
+        for h in range(2):
+            grouped = sb("grouped%d" % h, [P, Q, PACK], BF16)
+            nc.vector.tensor_copy(
+                out=grouped[:].rearrange("p (c i) j -> p c j i", i=4),
+                in_=raw[h][:].rearrange("p j (c i) -> p c j i", i=4),
+            )
+            codes = sb("q_codes%d" % h, [P, Q], U32)
+            scales = sb("q_scales%d" % h, [P, Q], U8)
+            nc.vector.quantize_mx(
+                out=codes[:].bitcast(FP8X4), scales=scales[:], in_=grouped[:].rearrange("p q j -> p (q j)")
+            )
+            q_codes.append(codes)
+            q_scales.append(scales)
+
+        def product(h, t0, width):
+            bank = psum.tile([P, width], F32, name="bank%d_%d" % (h, t0))
+            k0 = t0 % HALF
+            nc.tensor.matmul_mx(
+                out=bank[:],
+                lhsT=q_codes[h][:].bitcast(FP8X4),
+                lhsT_scale=q_scales[h][:],
+                rhs=key_codes[t0 // HALF][:, k0 : k0 + width].bitcast(FP8X4),
+                rhs_scale=key_scales[:, t0 : t0 + width],
+                start=True,
+                stop=True,
+            )
+            return bank
+
+        a = sb("a", [P, T])
+        b = sb("b", [P, T])
+        QUART = T // 4
+        nc.scalar.copy(out=a[:, 0:HALF], in_=product(0, 0, HALF)[:])
+        nc.vector.tensor_copy(out=a[:, HALF : HALF + QUART], in_=product(0, HALF, QUART)[:])
+        nc.scalar.copy(out=a[:, HALF + QUART : T], in_=product(0, HALF + QUART, QUART)[:])
+        bank_b0 = product(1, 0, HALF)
+        bank_b1 = product(1, HALF, HALF)
+
+        A1, A2, B1, B2 = range(4)
+        picked = sb("picked", [P, 4, I])
+        nc.vector.tensor_copy(picked[:, A1, :], a[:].indirect(list1[:]))
+        nc.scalar.activation(picked[:, A2, :], a[:].indirect(list2[:]), ACT.Copy)
+        nc.vector.tensor_copy(out=b[:, 0:HALF], in_=bank_b0[:])
+        nc.scalar.copy(out=b[:, HALF:T], in_=bank_b1[:])
+        nc.vector.tensor_copy(picked[:, B1, :], b[:].indirect(list1[:]))
+        nc.scalar.activation(picked[:, B2, :], b[:].indirect(list2[:]), ACT.Copy)
+
+        gain_r = sb("gain_r", [P, I])
+        gain_r2 = sb("gain_r2", [P, I])
+        share_m1 = sb("share_m1", [P, 1])
+        neg_sharp = sb("neg_sharp", [P, 1])
+        nc.gpsimd.tensor_scalar(share_m1[:], share_col[:], -1.0, 256.0, ALU.add, ALU.mult)
+        nc.gpsimd.tensor_scalar(gain_r[:], gain[:], share_col[:], 256.0, ALU.mult, ALU.mult)
+        nc.gpsimd.tensor_scalar(gain_r2[:], gain[:], share_m1[:], 1.0, ALU.mult, ALU.mult)
+        nc.gpsimd.tensor_scalar(neg_sharp[:], sharp_col[:], -1.0, 1.0, ALU.mult, ALU.mult)
+
+        squares, lengths = sb("squares", [P, 4, I]), sb("lengths", [P, 2, I])
+        prod, inv = sb("prod", [P, I]), sb("inv", [P, I])
+        runs = (slice(0, 256), slice(256, 384), slice(384, 512))
+        for run in runs:
+            nc.scalar.activation(squares[:, :, run], picked[:, :, run], ACT.Square)
+        for run in runs:
+            nc.vector.tensor_tensor(lengths[:, :, run], squares[:, 0:2, run], squares[:, 2:4, run], ALU.add)
+            nc.vector.tensor_tensor(prod[:, run], lengths[:, 0, run], lengths[:, 1, run], ALU.mult)
+            nc.scalar.activation(inv[:, run], prod[:, run], ACT.Abs_reciprocal_sqrt, bias=half_col[:])
+
+        pa, pb, dot, s, neg_s2 = sb("pa", [P, I]), sb("pb", [P, I]), sb("dot", [P, I]), sb("s", [P, I]), sb("neg_s2", [P, I])
+        nc.vector.tensor_tensor(pa[:], picked[:, A1, :], picked[:, A2, :], ALU.mult)
+        nc.vector.tensor_tensor(pb[:], picked[:, B1, :], picked[:, B2, :], ALU.mult)
+        nc.vector.tensor_tensor(dot[:], pa[:], pb[:], ALU.add)
+        for run in (slice(0, 256), slice(256, 512)):
+            nc.vector.scalar_tensor_tensor(s[:, run], dot[:, run], lam_col[:], inv[:, run], ALU.mult, ALU.mult)
+        neg_max = sb("neg_max", [P, 1])
+        neg_max2 = sb("neg_max2", [P, 1])
+        nc.vector.tensor_reduce(neg_max[:], s[:], AX.X, ALU.max, negate=True)
+        nc.vector.tensor_scalar(neg_s2[:], s[:], neg_sharp[:], None, ALU.mult, ALU.min, accum_out=neg_max2[:])
+
+        p, p2 = sb("p", [P, I]), sb("p2", [P, I])
+        total, total2 = sb("total", [P, 1]), sb("total2", [P, 1])
+        nc.scalar.activation(p[:], s[:], ACT.Exp, bias=neg_max[:], accum_out=total[:])
+        nc.scalar.activation(p2[:], neg_s2[:], ACT.Exp, bias=neg_max2[:], scale=-1.0, accum_out=total2[:])
+        rec, rec2 = sb("rec", [P, 1]), sb("rec2", [P, 1])
+        term, term2 = sb("term", [P, I]), sb("term2", [P, I])
+        nc.vector.reciprocal(rec[:], total[:])
+        nc.vector.scalar_tensor_tensor(term[:], p[:], rec[:], gain_r[:], ALU.mult, ALU.mult)
+        nc.vector.reciprocal(rec2[:], total2[:])
+        nc.vector.scalar_tensor_tensor(term2[:], p2[:], rec2[:], gain_r2[:], ALU.mult, ALU.mult)
+        nc.vector.tensor_tensor(placed[:].indirect(list4[:]), term[:], term2[:], ALU.add)
+
+        for h, queue in enumerate((nc.sync, nc.scalar)):
+            cols = slice(h * HALF, (h + 1) * HALF)
+            result = sb("result%d" % h, [P, HALF])
+            nc.vector.tensor_tensor(result[:], placed[:, cols], old_sb[:, cols], ALU.add)
+            queue.dma_start(out=out[:, cols], in_=result[:])

@@ -68,6 +68,8 @@ def tile_attend_planecos_twoheats_moved_heads_kernel(
         nc.vector.memset(placed[:], 0.0)
         half_col = sb("half_col", [P, 1])
         nc.vector.memset(half_col[:], 0.5)
+        warm = sb("warm", [P, 1])
+        nc.scalar.activation(warm[:], half_col[:], ACT.Abs_reciprocal_sqrt, bias=half_col[:])
 
         q_codes, q_scales = [], []
         for h in range(2):

@@ -29,20 +29,21 @@ def tile_attend_planecos_twoheats_moved_heads_kernel(
         pool = ctx.enter_context(tc.tile_pool(name="held", bufs=1))
         psum = ctx.enter_context(tc.psum_pool(name="psum", bufs=1))
 
-        def sb(name, shape, dtype=F32):
-            return pool.tile(shape, dtype, name=name, align_bytes=64)
+        def sb(name, shape, dtype=F32, tag=None):
+            return pool.tile(shape, dtype, name=name, tag=tag or name, align_bytes=64)
 
         key_scales = sb("key_scales", [P, T], U8)
-        for quad in range(4):
-            nc.scalar.dma_start(
-                out=key_scales[32 * quad : 32 * quad + 4, :].bitcast(I32),
-                in_=keys_scales[0, 4 * quad : 4 * quad + 4, :].bitcast(I32),
-            )
         key_bytes = keys_words[0].rearrange("p n t -> p (n t)")
         raw = [sb("raw_a", [P, PACK, Q]), sb("raw_b", [P, PACK, Q])]
         key_codes = [sb("key_codes_lo", [P, HALF], U32), sb("key_codes_hi", [P, HALF], U32)]
         for h, src in enumerate((query, query2)):
             nc.sync.dma_start(out=raw[h][:], in_=src.rearrange("(p j) q -> p j q", j=PACK))
+            if h == 0:
+                for quad in range(4):
+                    nc.sync.dma_start(
+                        out=key_scales[32 * quad : 32 * quad + 4, :].bitcast(I32),
+                        in_=keys_scales[0, 4 * quad : 4 * quad + 4, :].bitcast(I32),
+                    )
             nc.sync.dma_start(
                 out=key_codes[h][:].bitcast(I32),
                 in_=key_bytes[:, h * HALF * PACK : (h + 1) * HALF * PACK].bitcast(I32),
@@ -60,9 +61,9 @@ def tile_attend_planecos_twoheats_moved_heads_kernel(
         share_col = sb("share_col", [P, 1])
         lam_col = sb("lam_col", [P, 1])
         sharp_col = sb("sharp_col", [P, 1])
-        nc.gpsimd.dma_start(out=share_col[:], in_=share)
-        nc.gpsimd.dma_start(out=lam_col[:], in_=lam)
-        nc.gpsimd.dma_start(out=sharp_col[:], in_=sharp)
+        nc.sync.dma_start(out=share_col[:], in_=share)
+        nc.sync.dma_start(out=lam_col[:], in_=lam)
+        nc.sync.dma_start(out=sharp_col[:], in_=sharp)
 
         placed = sb("placed", [P, T])
         nc.vector.memset(placed[:], 0.0)
@@ -73,7 +74,7 @@ def tile_attend_planecos_twoheats_moved_heads_kernel(
 
         q_codes, q_scales = [], []
         for h in range(2):
-            grouped = sb("grouped%d" % h, [P, Q, PACK], BF16)
+            grouped = sb("grouped%d" % h, [P, Q, PACK], BF16, tag="grouped")
             nc.vector.tensor_copy(
                 out=grouped[:].rearrange("p (c i) j -> p c j i", i=4),
                 in_=raw[h][:].rearrange("p j (c i) -> p c j i", i=4),
@@ -106,59 +107,62 @@ def tile_attend_planecos_twoheats_moved_heads_kernel(
         nc.scalar.copy(out=a[:, 0:HALF], in_=product(0, 0, HALF)[:])
         nc.vector.tensor_copy(out=a[:, HALF : HALF + QUART], in_=product(0, HALF, QUART)[:])
         nc.scalar.copy(out=a[:, HALF + QUART : T], in_=product(0, HALF + QUART, QUART)[:])
-        bank_b0 = product(1, 0, HALF)
-        bank_b1 = product(1, HALF, HALF)
+        for t0 in range(0, T, QUART):
+            nc.vector.tensor_copy(out=b[:, t0 : t0 + QUART], in_=product(1, t0, QUART)[:])
 
-        A1, A2, B1, B2 = range(4)
-        picked = sb("picked", [P, 4, I])
-        nc.vector.tensor_copy(picked[:, A1, :], a[:].indirect(list1[:]))
-        nc.scalar.activation(picked[:, A2, :], a[:].indirect(list2[:]), ACT.Copy)
-        nc.vector.tensor_copy(out=b[:, 0:HALF], in_=bank_b0[:])
-        nc.scalar.copy(out=b[:, HALF:T], in_=bank_b1[:])
-        nc.vector.tensor_copy(picked[:, B1, :], b[:].indirect(list1[:]))
-        nc.scalar.activation(picked[:, B2, :], b[:].indirect(list2[:]), ACT.Copy)
-
-        gain_r = sb("gain_r", [P, I])
-        gain_r2 = sb("gain_r2", [P, I])
-        share_m1 = sb("share_m1", [P, 1])
-        neg_sharp = sb("neg_sharp", [P, 1])
-        nc.gpsimd.tensor_scalar(share_m1[:], share_col[:], -1.0, 256.0, ALU.add, ALU.mult)
-        nc.gpsimd.tensor_scalar(gain_r[:], gain[:], share_col[:], 256.0, ALU.mult, ALU.mult)
-        nc.gpsimd.tensor_scalar(gain_r2[:], gain[:], share_m1[:], 1.0, ALU.mult, ALU.mult)
-        nc.gpsimd.tensor_scalar(neg_sharp[:], sharp_col[:], -1.0, 1.0, ALU.mult, ALU.mult)
-
-        squares, lengths = sb("squares", [P, 4, I]), sb("lengths", [P, 2, I])
-        prod, inv = sb("prod", [P, I]), sb("inv", [P, I])
-        runs = (slice(0, 256), slice(256, 384), slice(384, 512))
+        a1, a2, b1, b2 = sb("a1", [P, I]), sb("a2", [P, I]), sb("b1", [P, I]), sb("b2", [P, I])
+        sq_a1, sq_a2, sq_b1, sq_b2 = sb("sq_a1", [P, I]), sb("sq_a2", [P, I]), sb("sq_b1", [P, I]), sb("sq_b2", [P, I])
+        runs = (slice(0, 256), slice(256, 512))
+        nc.vector.tensor_copy(a1[:], a[:].indirect(list1[:]))
+        nc.scalar.activation(a2[:], a[:].indirect(list2[:]), ACT.Copy)
+        nc.scalar.activation(sq_a2[:], a2[:], ACT.Square)
+        nc.scalar.activation(sq_a1[:], a1[:], ACT.Square)
+        nc.vector.tensor_copy(b1[:], b[:].indirect(list1[:]))
+        nc.scalar.activation(b2[:], b[:].indirect(list2[:]), ACT.Copy)
+        nc.scalar.activation(sq_b2[:], b2[:], ACT.Square)
         for run in runs:
-            nc.scalar.activation(squares[:, :, run], picked[:, :, run], ACT.Square)
-        for run in runs:
-            nc.vector.tensor_tensor(lengths[:, :, run], squares[:, 0:2, run], squares[:, 2:4, run], ALU.add)
-            nc.vector.tensor_tensor(prod[:, run], lengths[:, 0, run], lengths[:, 1, run], ALU.mult)
+            nc.scalar.activation(sq_b1[:, run], b1[:, run], ACT.Square)
+
+        share_r2 = sb("share_r2", [P, 1])
+        nc.gpsimd.tensor_scalar(share_r2[:], share_col[:], -1.0, 256.0, ALU.add, ALU.mult)
+
+        lb, prod, inv = sb("lb", [P, I]), sb("prod", [P, I]), sb("inv", [P, I])
+        la = [sb("la%d" % r, [P, I // 2]) for r in range(2)]
+        nc.vector.tensor_tensor(lb[:], sq_a2[:], sq_b2[:], ALU.add)
+        for r, run in enumerate(runs):
+            nc.vector.tensor_tensor(la[r][:], sq_a1[:, run], sq_b1[:, run], ALU.add)
+        for r, run in enumerate(runs):
+            nc.vector.tensor_tensor(prod[:, run], la[r][:], lb[:, run], ALU.mult)
             nc.scalar.activation(inv[:, run], prod[:, run], ACT.Abs_reciprocal_sqrt, bias=half_col[:])
 
-        pa, pb, dot, s, neg_s2 = sb("pa", [P, I]), sb("pb", [P, I]), sb("dot", [P, I]), sb("s", [P, I]), sb("neg_s2", [P, I])
-        nc.vector.tensor_tensor(pa[:], picked[:, A1, :], picked[:, A2, :], ALU.mult)
-        nc.vector.tensor_tensor(pb[:], picked[:, B1, :], picked[:, B2, :], ALU.mult)
-        nc.vector.tensor_tensor(dot[:], pa[:], pb[:], ALU.add)
-        for run in (slice(0, 256), slice(256, 512)):
-            nc.vector.scalar_tensor_tensor(s[:, run], dot[:, run], lam_col[:], inv[:, run], ALU.mult, ALU.mult)
+        pa, pb = sb("pa", [P, I]), sb("pb", [P, I])
+        neg_s, neg_s2 = sb("neg_s", [P, I]), sb("neg_s2", [P, I])
+        nc.vector.tensor_tensor(pa[:], a1[:], a2[:], ALU.mult)
+        nc.vector.tensor_tensor(pb[:], b1[:], b2[:], ALU.mult)
+        neg_dot = [sb("neg_dot%d" % r, [P, I // 2], tag="la%d" % r) for r in range(2)]
+        for r, run in enumerate(runs):
+            nc.vector.scalar_tensor_tensor(neg_dot[r][:], pa[:, run], -1.0, pb[:, run], ALU.mult, ALU.subtract)
+        for r, run in enumerate(runs):
+            nc.vector.scalar_tensor_tensor(neg_s[:, run], neg_dot[r][:], lam_col[:], inv[:, run], ALU.mult, ALU.mult)
         neg_max = sb("neg_max", [P, 1])
         neg_max2 = sb("neg_max2", [P, 1])
-        nc.vector.tensor_reduce(neg_max[:], s[:], AX.X, ALU.max, negate=True)
-        nc.vector.tensor_scalar(neg_s2[:], s[:], neg_sharp[:], None, ALU.mult, ALU.min, accum_out=neg_max2[:])
+        nc.vector.tensor_reduce(neg_max[:], neg_s[:], AX.X, ALU.min)
+        nc.vector.tensor_scalar(neg_s2[:], neg_s[:], sharp_col[:], None, ALU.mult, ALU.min, accum_out=neg_max2[:])
 
         p, p2 = sb("p", [P, I]), sb("p2", [P, I])
         total, total2 = sb("total", [P, 1]), sb("total2", [P, 1])
-        nc.scalar.activation(p[:], s[:], ACT.Exp, bias=neg_max[:], accum_out=total[:])
+        nc.scalar.activation(p[:], neg_s[:], ACT.Exp, bias=neg_max[:], scale=-1.0, accum_out=total[:])
         nc.scalar.activation(p2[:], neg_s2[:], ACT.Exp, bias=neg_max2[:], scale=-1.0, accum_out=total2[:])
         rec, rec2 = sb("rec", [P, 1]), sb("rec2", [P, 1])
-        term, term2 = sb("term", [P, I]), sb("term2", [P, I])
+        term, factor2, weight = sb("term", [P, I]), sb("factor2", [P, 1]), sb("weight", [P, I])
         nc.vector.reciprocal(rec[:], total[:])
-        nc.vector.scalar_tensor_tensor(term[:], p[:], rec[:], gain_r[:], ALU.mult, ALU.mult)
+        factor = sb("factor", [P, 1])
+        nc.vector.tensor_scalar(factor[:], rec[:], share_col[:], 256.0, ALU.mult, ALU.mult)
         nc.vector.reciprocal(rec2[:], total2[:])
-        nc.vector.scalar_tensor_tensor(term2[:], p2[:], rec2[:], gain_r2[:], ALU.mult, ALU.mult)
-        nc.vector.tensor_tensor(placed[:].indirect(list4[:]), term[:], term2[:], ALU.add)
+        nc.vector.tensor_scalar(factor2[:], rec2[:], share_r2[:], None, ALU.mult)
+        nc.vector.tensor_scalar(term[:], p[:], factor[:], None, ALU.mult)
+        nc.vector.scalar_tensor_tensor(weight[:], p2[:], factor2[:], term[:], ALU.mult, ALU.add)
+        nc.vector.tensor_tensor(placed[:].indirect(list4[:]), weight[:], gain[:], ALU.mult)
 
         for h, queue in enumerate((nc.sync, nc.scalar)):
             cols = slice(h * HALF, (h + 1) * HALF)

@@ -35,7 +35,8 @@ def tile_attend_planecos_twoheats_moved_heads_kernel(
         key_scales = sb("key_scales", [P, T], U8)
         key_bytes = keys_words[0].rearrange("p n t -> p (n t)")
         raw = [sb("raw_a", [P, PACK, Q]), sb("raw_b", [P, PACK, Q])]
-        key_codes = [sb("key_codes_lo", [P, HALF], U32), sb("key_codes_hi", [P, HALF], U32)]
+        key_cut = (0, 3 * T // 4, T)
+        key_codes = [sb("key_codes%d" % h, [P, key_cut[h + 1] - key_cut[h]], U32) for h in range(2)]
         for h, src in enumerate((query, query2)):
             nc.sync.dma_start(out=raw[h][:], in_=src.rearrange("(p j) q -> p j q", j=PACK))
             if h == 0:
@@ -46,7 +47,7 @@ def tile_attend_planecos_twoheats_moved_heads_kernel(
                     )
             nc.sync.dma_start(
                 out=key_codes[h][:].bitcast(I32),
-                in_=key_bytes[:, h * HALF * PACK : (h + 1) * HALF * PACK].bitcast(I32),
+                in_=key_bytes[:, key_cut[h] * PACK : key_cut[h + 1] * PACK].bitcast(I32),
             )
         list1 = pool.tile([P, I // 16], U16, name="list1")
         list2 = pool.tile([P, I // 16], U16, name="list2")
@@ -75,26 +76,32 @@ def tile_attend_planecos_twoheats_moved_heads_kernel(
         q_codes, q_scales = [], []
         for h in range(2):
             grouped = sb("grouped%d" % h, [P, Q, PACK], BF16, tag="grouped")
-            nc.vector.tensor_copy(
-                out=grouped[:].rearrange("p (c i) j -> p c j i", i=4),
-                in_=raw[h][:].rearrange("p j (c i) -> p c j i", i=4),
-            )
             codes = sb("q_codes%d" % h, [P, Q], U32)
             scales = sb("q_scales%d" % h, [P, Q], U8)
-            nc.vector.quantize_mx(
-                out=codes[:].bitcast(FP8X4), scales=scales[:], in_=grouped[:].rearrange("p q j -> p (q j)")
-            )
+            halves = (slice(0, Q // 2), slice(Q // 2, Q))
+            for cols in halves:
+                nc.vector.tensor_copy(
+                    out=grouped[:, cols, :].rearrange("p (c i) j -> p c j i", i=4),
+                    in_=raw[h][:, :, cols].rearrange("p j (c i) -> p c j i", i=4),
+                )
+            for cols in halves:
+                nc.vector.quantize_mx(
+                    out=codes[:, cols].bitcast(FP8X4),
+                    scales=scales[:, cols],
+                    in_=grouped[:, cols, :].rearrange("p q j -> p (q j)"),
+                )
             q_codes.append(codes)
             q_scales.append(scales)
 
         def product(h, t0, width):
             bank = psum.tile([P, width], F32, name="bank%d_%d" % (h, t0))
-            k0 = t0 % HALF
+            part = 0 if t0 < key_cut[1] else 1
+            k0 = t0 - key_cut[part]
             nc.tensor.matmul_mx(
                 out=bank[:],
                 lhsT=q_codes[h][:].bitcast(FP8X4),
                 lhsT_scale=q_scales[h][:],
-                rhs=key_codes[t0 // HALF][:, k0 : k0 + width].bitcast(FP8X4),
+                rhs=key_codes[part][:, k0 : k0 + width].bitcast(FP8X4),
                 rhs_scale=key_scales[:, t0 : t0 + width],
                 start=True,
                 stop=True,
@@ -105,8 +112,8 @@ def tile_attend_planecos_twoheats_moved_heads_kernel(
         b = sb("b", [P, T])
         QUART = T // 4
         nc.scalar.copy(out=a[:, 0:HALF], in_=product(0, 0, HALF)[:])
-        nc.vector.tensor_copy(out=a[:, HALF : HALF + QUART], in_=product(0, HALF, QUART)[:])
-        nc.scalar.copy(out=a[:, HALF + QUART : T], in_=product(0, HALF + QUART, QUART)[:])
+        nc.scalar.copy(out=a[:, HALF : HALF + QUART], in_=product(0, HALF, QUART)[:])
+        nc.vector.tensor_copy(out=a[:, HALF + QUART : T], in_=product(0, HALF + QUART, QUART)[:])
         for t0 in range(0, T, QUART):
             nc.vector.tensor_copy(out=b[:, t0 : t0 + QUART], in_=product(1, t0, QUART)[:])
 
@@ -123,7 +130,9 @@ def tile_attend_planecos_twoheats_moved_heads_kernel(
         for run in runs:
             nc.scalar.activation(sq_b1[:, run], b1[:, run], ACT.Square)
 
+        share_r = sb("share_r", [P, 1])
         share_r2 = sb("share_r2", [P, 1])
+        nc.gpsimd.tensor_scalar(share_r[:], share_col[:], 256.0, 0.0, ALU.mult, ALU.add)
         nc.gpsimd.tensor_scalar(share_r2[:], share_col[:], -1.0, 256.0, ALU.add, ALU.mult)
 
         lb, prod, inv = sb("lb", [P, I]), sb("prod", [P, I]), sb("inv", [P, I])
@@ -156,16 +165,15 @@ def tile_attend_planecos_twoheats_moved_heads_kernel(
         rec, rec2 = sb("rec", [P, 1]), sb("rec2", [P, 1])
         term, factor2, weight = sb("term", [P, I]), sb("factor2", [P, 1]), sb("weight", [P, I])
         nc.vector.reciprocal(rec[:], total[:])
-        factor = sb("factor", [P, 1])
-        nc.vector.tensor_scalar(factor[:], rec[:], share_col[:], 256.0, ALU.mult, ALU.mult)
+        nc.vector.tensor_scalar(term[:], p[:], rec[:], share_r[:], ALU.mult, ALU.mult)
         nc.vector.reciprocal(rec2[:], total2[:])
         nc.vector.tensor_scalar(factor2[:], rec2[:], share_r2[:], None, ALU.mult)
-        nc.vector.tensor_scalar(term[:], p[:], factor[:], None, ALU.mult)
         nc.vector.scalar_tensor_tensor(weight[:], p2[:], factor2[:], term[:], ALU.mult, ALU.add)
         nc.vector.tensor_tensor(placed[:].indirect(list4[:]), weight[:], gain[:], ALU.mult)
 
-        for h, queue in enumerate((nc.sync, nc.scalar)):
-            cols = slice(h * HALF, (h + 1) * HALF)
-            result = sb("result%d" % h, [P, HALF])
+        cuts = (0, 384, 768, T)
+        for h, queue in enumerate((nc.sync, nc.scalar, nc.sync)):
+            cols = slice(cuts[h], cuts[h + 1])
+            result = sb("result%d" % h, [P, cuts[h + 1] - cuts[h]])
             nc.vector.tensor_tensor(result[:], placed[:, cols], old_sb[:, cols], ALU.add)
             queue.dma_start(out=out[:, cols], in_=result[:])

from contextlib import ExitStack

import concourse.mybir as mybir

F32 = mybir.dt.float32
BF16 = mybir.dt.bfloat16
I32 = mybir.dt.int32
U32 = mybir.dt.uint32
U16 = mybir.dt.uint16
U8 = mybir.dt.uint8
FP8X4 = mybir.dt.float8_e4m3fn_x4
ALU = mybir.AluOpType
ACT = mybir.ActivationFunctionType
AX = mybir.AxisListType

P = 128
PACK = 4
D, T, I, Q = 512, 1024, 512, 128
HALF = T // 2

FLOPS = 2 * 2 * D * Q * T


def tile_attend_planecos_twoheats_moved_heads_kernel(
    tc, query, query2, keys_words, keys_scales, lam, sharp, share, old, gainm, offs, offs2, offs4, out
):
    nc = tc.nc
    with ExitStack() as ctx:
        pool = ctx.enter_context(tc.tile_pool(name="held", bufs=1))
        psum = ctx.enter_context(tc.psum_pool(name="psum", bufs=1))

        def sb(name, shape, dtype=F32, tag=None):
            return pool.tile(shape, dtype, name=name, tag=tag or name, align_bytes=64)

        key_scales = sb("key_scales", [P, T], U8)
        key_bytes = keys_words[0].rearrange("p n t -> p (n t)")
        raw = [sb("raw_a", [P, PACK, Q]), sb("raw_b", [P, PACK, Q])]
        key_cut = (0, 3 * T // 4, T)
        key_codes = [sb("key_codes%d" % h, [P, key_cut[h + 1] - key_cut[h]], U32) for h in range(2)]
        for h, src in enumerate((query, query2)):
            nc.sync.dma_start(out=raw[h][:], in_=src.rearrange("(p j) q -> p j q", j=PACK))
            if h == 0:
                for quad in range(4):
                    nc.sync.dma_start(
                        out=key_scales[32 * quad : 32 * quad + 4, :].bitcast(I32),
                        in_=keys_scales[0, 4 * quad : 4 * quad + 4, :].bitcast(I32),
                    )
            nc.sync.dma_start(
                out=key_codes[h][:].bitcast(I32),
                in_=key_bytes[:, key_cut[h] * PACK : key_cut[h + 1] * PACK].bitcast(I32),
            )
        list1 = pool.tile([P, I // 16], U16, name="list1")
        list2 = pool.tile([P, I // 16], U16, name="list2")
        list4 = pool.tile([P, I // 16], U16, name="list4")
        nc.sync.dma_start(list1[:], offs)
        nc.sync.dma_start(list2[:], offs2)
        gain = sb("gain", [P, I])
        nc.sync.dma_start(out=gain[:], in_=gainm)
        nc.sync.dma_start(list4[:], offs4)
        old_sb = sb("old_sb", [P, T])
        nc.sync.dma_start(out=old_sb[:], in_=old)
        share_col = sb("share_col", [P, 1])
        lam_col = sb("lam_col", [P, 1])
        sharp_col = sb("sharp_col", [P, 1])
        nc.sync.dma_start(out=share_col[:], in_=share)
        nc.sync.dma_start(out=lam_col[:], in_=lam)
        nc.sync.dma_start(out=sharp_col[:], in_=sharp)

        placed = sb("placed", [P, T])
        nc.vector.memset(placed[:], 0.0)
        half_col = sb("half_col", [P, 1])
        nc.vector.memset(half_col[:], 0.5)
        warm = sb("warm", [P, 1])
        nc.scalar.activation(warm[:], half_col[:], ACT.Abs_reciprocal_sqrt, bias=half_col[:])

        q_codes, q_scales = [], []
        for h in range(2):
            grouped = sb("grouped%d" % h, [P, Q, PACK], BF16, tag="grouped")
            codes = sb("q_codes%d" % h, [P, Q], U32)
            scales = sb("q_scales%d" % h, [P, Q], U8)
            halves = (slice(0, Q // 2), slice(Q // 2, Q))
            for cols in halves:
                nc.vector.tensor_copy(
                    out=grouped[:, cols, :].rearrange("p (c i) j -> p c j i", i=4),
                    in_=raw[h][:, :, cols].rearrange("p j (c i) -> p c j i", i=4),
                )
            for cols in halves:
                nc.vector.quantize_mx(
                    out=codes[:, cols].bitcast(FP8X4),
                    scales=scales[:, cols],
                    in_=grouped[:, cols, :].rearrange("p q j -> p (q j)"),
                )
            q_codes.append(codes)
            q_scales.append(scales)

        def product(h, t0, width):
            bank = psum.tile([P, width], F32, name="bank%d_%d" % (h, t0))
            part = 0 if t0 < key_cut[1] else 1
            k0 = t0 - key_cut[part]
            nc.tensor.matmul_mx(
                out=bank[:],
                lhsT=q_codes[h][:].bitcast(FP8X4),
                lhsT_scale=q_scales[h][:],
                rhs=key_codes[part][:, k0 : k0 + width].bitcast(FP8X4),
                rhs_scale=key_scales[:, t0 : t0 + width],
                start=True,
                stop=True,
            )
            return bank

        a = sb("a", [P, T])
        b = sb("b", [P, T])
        QUART = T // 4
        nc.scalar.copy(out=a[:, 0:HALF], in_=product(0, 0, HALF)[:])
        nc.scalar.copy(out=a[:, HALF : HALF + QUART], in_=product(0, HALF, QUART)[:])
        nc.vector.tensor_copy(out=a[:, HALF + QUART : T], in_=product(0, HALF + QUART, QUART)[:])
        for t0 in range(0, T, QUART):
            nc.vector.tensor_copy(out=b[:, t0 : t0 + QUART], in_=product(1, t0, QUART)[:])

        a1, a2, b1, b2 = sb("a1", [P, I]), sb("a2", [P, I]), sb("b1", [P, I]), sb("b2", [P, I])
        sq_a1, sq_a2, sq_b1, sq_b2 = sb("sq_a1", [P, I]), sb("sq_a2", [P, I]), sb("sq_b1", [P, I]), sb("sq_b2", [P, I])
        runs = (slice(0, 256), slice(256, 512))
        nc.vector.tensor_copy(a1[:], a[:].indirect(list1[:]))
        nc.scalar.activation(a2[:], a[:].indirect(list2[:]), ACT.Copy)
        nc.scalar.activation(sq_a2[:], a2[:], ACT.Square)
        nc.scalar.activation(sq_a1[:], a1[:], ACT.Square)
        nc.vector.tensor_copy(b1[:], b[:].indirect(list1[:]))
        nc.scalar.activation(b2[:], b[:].indirect(list2[:]), ACT.Copy)
        nc.scalar.activation(sq_b2[:], b2[:], ACT.Square)
        for run in runs:
            nc.scalar.activation(sq_b1[:, run], b1[:, run], ACT.Square)

        share_r = sb("share_r", [P, 1])
        share_r2 = sb("share_r2", [P, 1])
        nc.gpsimd.tensor_scalar(share_r[:], share_col[:], 256.0, 0.0, ALU.mult, ALU.add)
        nc.gpsimd.tensor_scalar(share_r2[:], share_col[:], -1.0, 256.0, ALU.add, ALU.mult)

        lb, prod, inv = sb("lb", [P, I]), sb("prod", [P, I]), sb("inv", [P, I])
        la = [sb("la%d" % r, [P, I // 2]) for r in range(2)]
        nc.vector.tensor_tensor(lb[:], sq_a2[:], sq_b2[:], ALU.add)
        for r, run in enumerate(runs):
            nc.vector.tensor_tensor(la[r][:], sq_a1[:, run], sq_b1[:, run], ALU.add)
        for r, run in enumerate(runs):
            nc.vector.tensor_tensor(prod[:, run], la[r][:], lb[:, run], ALU.mult)
            nc.scalar.activation(inv[:, run], prod[:, run], ACT.Abs_reciprocal_sqrt, bias=half_col[:])

        pa, pb = sb("pa", [P, I]), sb("pb", [P, I])
        neg_s, neg_s2 = sb("neg_s", [P, I]), sb("neg_s2", [P, I])
        nc.vector.tensor_tensor(pa[:], a1[:], a2[:], ALU.mult)
        nc.vector.tensor_tensor(pb[:], b1[:], b2[:], ALU.mult)
        neg_dot = [sb("neg_dot%d" % r, [P, I // 2], tag="la%d" % r) for r in range(2)]
        for r, run in enumerate(runs):
            nc.vector.scalar_tensor_tensor(neg_dot[r][:], pa[:, run], -1.0, pb[:, run], ALU.mult, ALU.subtract)
        for r, run in enumerate(runs):
            nc.vector.scalar_tensor_tensor(neg_s[:, run], neg_dot[r][:], lam_col[:], inv[:, run], ALU.mult, ALU.mult)
        neg_max = sb("neg_max", [P, 1])
        neg_max2 = sb("neg_max2", [P, 1])
        nc.vector.tensor_reduce(neg_max[:], neg_s[:], AX.X, ALU.min)
        nc.vector.tensor_scalar(neg_s2[:], neg_s[:], sharp_col[:], None, ALU.mult, ALU.min, accum_out=neg_max2[:])

        p, p2 = sb("p", [P, I]), sb("p2", [P, I])
        total, total2 = sb("total", [P, 1]), sb("total2", [P, 1])
        nc.scalar.activation(p[:], neg_s[:], ACT.Exp, bias=neg_max[:], scale=-1.0, accum_out=total[:])
        nc.scalar.activation(p2[:], neg_s2[:], ACT.Exp, bias=neg_max2[:], scale=-1.0, accum_out=total2[:])
        rec, rec2 = sb("rec", [P, 1]), sb("rec2", [P, 1])
        term, factor2, weight = sb("term", [P, I]), sb("factor2", [P, 1]), sb("weight", [P, I])
        nc.vector.reciprocal(rec[:], total[:])
        nc.vector.tensor_scalar(term[:], p[:], rec[:], share_r[:], ALU.mult, ALU.mult)
        nc.vector.reciprocal(rec2[:], total2[:])
        nc.vector.tensor_scalar(factor2[:], rec2[:], share_r2[:], None, ALU.mult)
        nc.vector.scalar_tensor_tensor(weight[:], p2[:], factor2[:], term[:], ALU.mult, ALU.add)
        nc.vector.tensor_tensor(placed[:].indirect(list4[:]), weight[:], gain[:], ALU.mult)

        cuts = (0, 384, 768, T)
        for h, queue in enumerate((nc.sync, nc.scalar, nc.sync)):
            cols = slice(cuts[h], cuts[h + 1])
            result = sb("result%d" % h, [P, cuts[h + 1] - cuts[h]])
            nc.vector.tensor_tensor(result[:], placed[:, cols], old_sb[:, cols], ALU.add)
            queue.dma_start(out=out[:, cols], in_=result[:])
